import numpy as np
import ml_dtypes


def mxq(x, axis, fmt="e4m3"):
    dtype, down = {"e4m3": (ml_dtypes.float8_e4m3fn, 7), "e5m2": (ml_dtypes.float8_e5m2, 14)}[fmt]
    v = np.moveaxis(np.asarray(x, np.float32).astype(ml_dtypes.bfloat16).astype(np.float64), axis, -1)
    blocks = v.reshape(v.shape[:-1] + (-1, 32))
    amax = np.abs(blocks).max(-1, keepdims=True)
    byte = np.maximum(np.where(amax > 0, np.frexp(amax)[1] - 1 + 127, 0) - down, 1)
    scale = np.exp2(byte - 127.0)
    codes = (blocks / scale).astype(np.float32).astype(dtype).astype(np.float64)
    return np.moveaxis((codes * scale).reshape(v.shape), -1, axis)


WIDE = False


def mx_kscale(k):
    if not WIDE:
        return np.ones(k)
    levels = np.array([10, -10, 5, -5, 0])
    if k % 512:
        return np.exp2(np.random.permutation(np.resize(levels, k // 32))).repeat(32)
    a = np.empty((k // 512, 16))
    for p in range(k // 512):
        a[p, :8] = np.random.permutation(np.resize(levels, 8))
        for g in range(8):
            far = levels[np.abs(levels - a[p, g]) >= 10]
            a[p, g + 8] = far[np.random.randint(len(far))]
    return np.exp2(a.ravel()).repeat(32)


def f64(x):
    return np.asarray(x).astype(np.float64)


def striped(idx):
    return np.tile(idx.reshape(-1, 16).T, (8, 1)).astype(np.uint16)


def unstriped(offs):
    return offs[:16].T.reshape(-1).astype(np.int64)


def striped8(idx):
    return np.concatenate([x.reshape(-1, 16).T for x in idx]).astype(np.uint16)


def runs(offs, k):
    lists = np.stack([offs[16 * r : 16 * r + 16].T.reshape(-1) for r in range(8)]).astype(np.int64)
    return lists[np.arange(k) % 512 // 64]


def pack_weight(w):
    k, n = w.shape
    w = f64(np.asarray(w, np.float32).astype(ml_dtypes.bfloat16)).reshape(k // 32, 32, n)
    amax = np.abs(w).max(1)
    byte = np.clip(np.where(amax > 0, np.frexp(amax)[1] - 1 + 127 - 7, 1), 1, 254)
    scaled = (w * np.exp2(127.0 - byte)[:, None, :]).reshape(k, n).astype(np.float32)
    words = np.ascontiguousarray(scaled.reshape(k // 512, 128, 4, n).transpose(0, 1, 3, 2)).astype(ml_dtypes.float8_e4m3fn).view(np.uint8)
    return words, np.ascontiguousarray(byte.astype(np.uint8).reshape(k // 512, 16, n))


def unpack_weight(words, scales):
    g, p, n, _ = words.shape
    vals = np.ascontiguousarray(words).view(ml_dtypes.float8_e4m3fn).astype(np.float64) * np.repeat(np.exp2(scales.astype(np.float64) - 127.0), 8, axis=1)[..., None]
    return vals.transpose(0, 1, 3, 2).reshape(g * 512, n)


E2M1 = np.array([0.0, 0.5, 1.0, 1.5, 2.0, 3.0, 4.0, 6.0, -0.0, -0.5, -1.0, -1.5, -2.0, -3.0, -4.0, -6.0])


def pack_fp4(w):
    k, n = w.shape
    w = f64(np.asarray(w, np.float32).astype(ml_dtypes.bfloat16)).reshape(k // 32, 32, n)
    amax = np.abs(w).max(1)
    mant, ex = np.frexp(amax / 6.0)
    byte = np.clip(np.where(amax > 0, np.where(mant > 0.5, ex, ex - 1) + 127, 1), 1, 254)
    scaled = (w * np.exp2(127.0 - byte)[:, None, :]).reshape(k, n).astype(np.float32)
    c = np.ascontiguousarray(scaled.reshape(k // 512, 128, 4, n).transpose(0, 1, 3, 2)).astype(ml_dtypes.float4_e2m1fn).view(np.uint8) & 0xF
    words = (c[..., 0::2] | (c[..., 1::2] << 4)).reshape(k // 512, 128, 2 * n)
    return np.ascontiguousarray(words), np.ascontiguousarray(byte.astype(np.uint8).reshape(k // 512, 16, n))


def unpack_fp4(words, scales):
    g, _, n = scales.shape
    words = np.ascontiguousarray(words).reshape(g, 128, n, 2)
    nib = np.empty((g, 128, n, 4), np.uint8)
    nib[..., 0::2] = words & 0xF
    nib[..., 1::2] = words >> 4
    vals = E2M1[nib] * np.repeat(np.exp2(scales.astype(np.float64) - 127.0), 8, axis=1)[..., None]
    return vals.transpose(0, 1, 3, 2).reshape(g * 512, n)


def sigmoid(v):
    return 1.0 / (1.0 + np.exp(-np.maximum(v, -700.0)))

def planes(y):
    n, m = y.shape
    v = y.astype(np.float32).astype(ml_dtypes.bfloat16).astype(np.float64).reshape(n // 32, 32, m)
    top = np.abs(v).max(1)
    byte = np.clip(np.where(top > 0, np.frexp(top)[1] - 1 + 127 - 7, 1), 1, 254)
    codes = (v * np.exp2(127.0 - byte)[:, None, :]).reshape(n, m).astype(np.float32).astype(ml_dtypes.float8_e4m3fn).view(np.uint8)
    words = codes.reshape(n // 512, 128, 4, m).transpose(0, 1, 3, 2)
    return np.ascontiguousarray(words), np.ascontiguousarray(byte.astype(np.uint8).reshape(n // 512, 16, m))


K, T, S, N, H = 512, 2048, 512, 512, 512


def setup_inputs():
    n = np.random.standard_normal
    s = mx_kscale(K)[:, None]
    u = mx_kscale(H)
    packed_xT = pack_weight(n((K, T)) * s)
    packed_w1 = pack_fp4(n((K, H)) / np.sqrt(K) / s)
    packed_w2 = pack_fp4(n((K, H)) / np.sqrt(K) / s)
    packed_w3 = pack_fp4(n((K, H)) / np.sqrt(K) / s)
    packed_w4 = pack_fp4(n((H, N)) / np.sqrt(H) / u[:, None])
    return {
        "x_words": packed_xT[0],
        "x_scales": packed_xT[1],
        "w1_words": packed_w1[0],
        "w1_scales": packed_w1[1],
        "w2_words": packed_w2[0],
        "w2_scales": packed_w2[1],
        "w3_words": packed_w3[0],
        "w3_scales": packed_w3[1],
        "gn": (np.random.uniform(0.5, 1.5, (H, 1)) * u[:, None]).astype(np.float32),
        "w4_words": packed_w4[0],
        "w4_scales": packed_w4[1],
        "offs": striped(np.random.permutation(T)[:S]),
        "two": striped(np.random.permutation(T)[:S]),
        "thr": striped(np.random.permutation(T)[:S]),
        "sym_l": striped8(np.random.randint(0, S, (8, S))),
        "del_l": striped8(np.stack([np.random.permutation(S) for _ in range(8)])),
        "ins_l": striped8(np.stack([np.random.permutation(S) for _ in range(8)])),
        "sub_l": striped8(np.stack([np.random.permutation(S) for _ in range(8)])),
    }


def reference(x_words, x_scales, w1_words, w1_scales, w2_words, w2_scales, w3_words, w3_scales, gn, w4_words, w4_scales, offs, two, thr, sym_l, del_l, ins_l, sub_l):
    xq = unpack_weight(x_words, x_scales)[:, unstriped(offs)]
    y = unpack_fp4(w1_words, w1_scales).T @ xq
    x_two = unpack_weight(x_words, x_scales)[:, unstriped(two)]
    c = unpack_fp4(w2_words, w2_scales).T @ x_two
    x_thr = unpack_weight(x_words, x_scales)[:, unstriped(thr)]
    d = unpack_fp4(w3_words, w3_scales).T @ x_thr
    sb = sigmoid(np.abs(c - (d[np.arange(H)[:, None], runs(sym_l, H)])))
    z = f64(gn) * (np.minimum(np.minimum(y[np.arange(H)[:, None], runs(del_l, H)] + 0.5, y[np.arange(H)[:, None], runs(ins_l, H)] + 0.5), y[np.arange(H)[:, None], runs(sub_l, H)] + sb))
    out_0 = unpack_fp4(w4_words, w4_scales).T @ mxq(z, 0, "e4m3")
    return (out_0,) + planes(out_0)

@@ -1,0 +1,246 @@
+from contextlib import ExitStack
+
+import concourse.mybir as mybir
+
+F32 = mybir.dt.float32
+BF16 = mybir.dt.bfloat16
+I32 = mybir.dt.int32
+U32 = mybir.dt.uint32
+U16 = mybir.dt.uint16
+U8 = mybir.dt.uint8
+FP8X4 = mybir.dt.float8_e4m3fn_x4
+FP4X4 = mybir.dt.float4_e2m1fn_x4
+ACT = mybir.ActivationFunctionType
+ALU = mybir.AluOpType
+
+P = 128
+PACK = 4
+T = 2048
+S = 512
+F = 512
+HALF = 256
+LIST_ROWS = 16
+CHUNKS = [(0, 128), (128, 128), (256, 128), (384, 128)]
+WIDEST = 128
+
+REUSE = {"c_x_words0": "w2_scale_raw", "y_x_words0": "w1_scale_raw", "bent0": "y_x_words1"}
+
+FLOPS = 4 * 2 * 512 * 512 * 512
+
+
+def tile_picked_editcell_none_po_kernel(
+    tc, x_words, x_scales, w1_words, w1_scales, w2_words, w2_scales, w3_words, w3_scales, gn,
+    w4_words, w4_scales, offs, two, thr, sym_l, del_l, ins_l, sub_l, out_0, out_1, out_2,
+):
+    nc = tc.nc
+    with ExitStack() as ctx:
+        keep = ctx.enter_context(tc.tile_pool(name="keep", bufs=1))
+        psum = ctx.enter_context(tc.psum_pool(name="psum", bufs=8))
+
+        def load_list(src, name):
+            tile = keep.tile([P, S // LIST_ROWS], U16, name=name)
+            nc.sync.dma_start(tile[:], src)
+            return tile
+
+        def entries(lst, start, width):
+            return lst[:, start // LIST_ROWS : (start + width) // LIST_ROWS]
+
+        def load_scale_rows_everywhere(queues, tile, src):
+            for q in range(4):
+                rows = src[0, 4 * q : 4 * q + 4, :].bitcast(I32)
+                queues[q].dma_start(tile[32 * q : 32 * q + 32, :].bitcast(I32), rows.unsqueeze(0).to_broadcast([8] + list(rows.shape)))
+
+        x_scale_table = keep.tile([P, T], U8, name="x_scale_table", align_bytes=64)
+        w_scale_raw = {}
+        for name in ("w1", "w3", "w2", "w4"):
+            w_scale_raw[name] = keep.tile([P, F], U8, name=name + "_scale_raw", tag=name + "_scale_raw", align_bytes=64)
+
+        def load_words(name, words):
+            raw = keep.tile([P, 2 * F], U8, name=name + "_word_raw", align_bytes=64)
+            nc.sync.dma_start(raw[:].bitcast(I32), words[0].bitcast(I32))
+            return raw
+
+        def deal_weight(name, raw):
+            words = keep.tile([P, 2 * F], U8, name=name + "_words", align_bytes=64)
+            nc.scalar.copy(
+                out=words[:].bitcast(U16).rearrange("p (t m) -> p t m", t=PACK),
+                in_=raw[:].bitcast(U16).rearrange("p (m t) -> p t m", t=PACK),
+            )
+            scales = keep.tile([P, F], U8, name=name + "_scales", align_bytes=64)
+            nc.vector.tensor_copy(
+                out=scales[:].rearrange("p (t m) -> p t m", t=PACK),
+                in_=w_scale_raw[name][:].rearrange("p (m t) -> p t m", t=PACK),
+            )
+            return words, scales
+
+        load_scale_rows_everywhere([nc.sync, nc.sync, nc.scalar, nc.scalar], x_scale_table, x_scales)
+        thr_t = load_list(thr, "thr_t")
+        w3_raw = load_words("w3", w3_words)
+        x_word_table = keep.tile([P, T], I32, name="x_word_table", tag="x_word_table", align_bytes=64)
+        nc.sync.dma_start(x_word_table[:], x_words[0].rearrange("p n t -> p (n t)").bitcast(I32))
+        load_scale_rows_everywhere([nc.sync] * 4, w_scale_raw["w3"], w3_scales)
+        w2_raw = load_words("w2", w2_words)
+        load_scale_rows_everywhere([nc.sync] * 4, w_scale_raw["w2"], w2_scales)
+        two_t = load_list(two, "two_t")
+        w1_raw = load_words("w1", w1_words)
+        gain = keep.tile([P, PACK], F32, name="gain")
+        nc.sync.dma_start(gain[:], gn.rearrange("(p t) o -> p (t o)", t=PACK))
+        load_scale_rows_everywhere([nc.sync] * 4, w_scale_raw["w1"], w1_scales)
+        offs_t = load_list(offs, "offs_t")
+        sym_t = load_list(sym_l, "sym_t")
+        w4_raw = load_words("w4", w4_words)
+        del_t = load_list(del_l, "del_t")
+        ins_t = load_list(ins_l, "ins_t")
+        sub_t = load_list(sub_l, "sub_t")
+        load_scale_rows_everywhere([nc.sync] * 4, w_scale_raw["w4"], w4_scales)
+
+        gain_size = keep.tile([P, PACK], F32, name="gain_size")
+        nc.scalar.activation(out=gain_size[:], in_=gain[:], func=ACT.Abs)
+        half_gain_size = keep.tile([P, PACK], F32, name="half_gain_size")
+        nc.scalar.activation(out=half_gain_size[:], in_=gain[:], func=ACT.Abs, scale=0.5)
+        gain_sign = keep.tile([P, WIDEST, PACK], BF16, name="gain_sign", align_bytes=64)
+        nc.scalar.activation(out=gain_sign[:], in_=gain[:].unsqueeze(1).to_broadcast([P, WIDEST, PACK]), func=ACT.Sign)
+
+        def product(weight, words, scales, width, name):
+            w_words, w_scales = weight
+            per_bank = 512 // width
+            results = []
+            for t0 in range(0, PACK, per_bank):
+                bank = psum.tile([P, per_bank, width], F32, name="bank")
+                for i in range(per_bank):
+                    t = t0 + i
+                    nc.tensor.matmul_mx(
+                        out=bank[:, i, :],
+                        lhsT=w_words[:, 2 * P * t : 2 * P * (t + 1)].bitcast(FP4X4),
+                        lhsT_scale=w_scales[:, P * t : P * (t + 1)],
+                        rhs=words.bitcast(FP8X4),
+                        rhs_scale=scales,
+                        start=True,
+                        stop=True,
+                    )
+                results.append((t0, per_bank, bank))
+            return results
+
+        def picked_product(lst, weight, name, empty):
+            scales = keep.tile([P, S], U8, name=name + "_x_scales", align_bytes=64)
+            nc.vector.tensor_copy(out=scales[:], in_=x_scale_table[:].indirect(lst[:]))
+            for h in range(S // HALF):
+                words = keep.tile([P, HALF], U32, name="%s_x_words%d" % (name, h), tag=REUSE.get("%s_x_words%d" % (name, h), "%s_x_words%d" % (name, h)), align_bytes=64)
+                nc.vector.tensor_copy(out=words[:], in_=x_word_table[:].bitcast(U32).indirect(entries(lst, h * HALF, HALF)))
+                for t0, count, bank in product(weight, words[:], scales[:, h * HALF : (h + 1) * HALF], HALF, name):
+                    empty(h, t0, count, bank)
+
+        y_rows = [keep.tile([P, S], F32, name="y_rows%d" % t) for t in range(PACK)]
+        d_rows = [keep.tile([P, S], F32, name="d_rows%d" % t) for t in range(PACK)]
+        c_rows = keep.tile([P, PACK, S], F32, name="c_rows")
+
+        def empty_y(h, t0, count, bank):
+            for i in range(count):
+                t = t0 + i
+                nc.scalar.activation(
+                    out=y_rows[t][:, h * HALF : (h + 1) * HALF], in_=bank[:, i, :], func=ACT.Identity,
+                    scale=gain_size[:, t : t + 1], bias=half_gain_size[:, t : t + 1],
+                )
+
+        def empty_d(h, t0, count, bank):
+            for i in range(count):
+                nc.scalar.copy(out=d_rows[t0 + i][:, h * HALF : (h + 1) * HALF], in_=bank[:, i, :])
+
+        def empty_c(h, t0, count, bank):
+            nc.scalar.copy(out=c_rows[:, t0 : t0 + count, h * HALF : (h + 1) * HALF], in_=bank[:])
+
+        picked_product(thr_t, deal_weight("w3", w3_raw), "d", empty_d)
+        picked_product(two_t, deal_weight("w2", w2_raw), "c", empty_c)
+        picked_product(offs_t, deal_weight("w1", w1_raw), "y", empty_y)
+        w4 = deal_weight("w4", w4_raw)
+
+        gaps = keep.tile([P, len(CHUNKS), PACK, WIDEST], F32, name="gaps", tag="x_word_table", align_bytes=64)
+        out_scales = keep.tile([P, S], U8, name="out_scales", align_bytes=64)
+        out_rows = out_0.rearrange("(p t) j -> p t j", t=PACK)
+        out_words = out_1[0].rearrange("p n t -> p (n t)").bitcast(I32)
+
+        def rows_tile(name, j0, width):
+            own = "%s%d" % (name, j0)
+            return keep.tile([P, PACK, width], F32, name=own, tag=REUSE.get(own, own), align_bytes=64)
+
+        def woven(ap):
+            return ap.rearrange("p (c i) t -> p c t i", i=4)
+
+        def unwoven(ap):
+            return ap.rearrange("p t (c i) -> p c t i", i=4)
+
+        def symbol_gap(j0, width):
+            gap = gaps[:, j0 // width, :, :]
+            for t in range(PACK):
+                nc.vector.tensor_tensor(
+                    out=gap[:, t, :], in0=d_rows[t][:].indirect(entries(sym_t, j0, width)),
+                    in1=c_rows[:, t, j0 : j0 + width], op=ALU.subtract,
+                )
+            return gap
+
+        def substitution_cost(gap, j0, width):
+            bent = rows_tile("bent", j0, width)
+            nc.scalar.activation(out=bent[:], in_=gap, func=ACT.Tanh, scale=0.5)
+            cost = rows_tile("cost", j0, width)
+            for t in range(PACK):
+                nc.scalar.activation(out=cost[:, t, :], in_=bent[:, t, :], func=ACT.Abs, scale=half_gain_size[:, t : t + 1])
+            return cost
+
+        def fetch(lst, name, j0, width):
+            got = rows_tile(name, j0, width)
+            for t in range(PACK):
+                window = y_rows[t][:].indirect(entries(lst, j0, width))
+                if (name, j0) == ("inserted", 384):
+                    nc.vector.tensor_copy(out=got[:, t, :], in_=window)
+                else:
+                    nc.scalar.activation(out=got[:, t, :], in_=window, func=ACT.Copy)
+            return got
+
+        def substituted(cost, j0, width):
+            got = rows_tile("sub", j0, width)
+            for t in range(PACK):
+                nc.vector.tensor_tensor(
+                    out=got[:, t, :], in0=y_rows[t][:].indirect(entries(sub_t, j0, width)), in1=cost[:, t, :], op=ALU.add,
+                )
+            return got
+
+        def quantise(values, j0, width, name, scales):
+            words = keep.tile([P, width], U32, name="%s_words%d" % (name, j0), align_bytes=64)
+            nc.vector.quantize_mx(out=words[:].bitcast(FP8X4), scales=scales, in_=values[:].rearrange("p j t -> p (j t)"))
+            return words
+
+        def cell(deleted, inserted, sub, j0, width):
+            lesser = rows_tile("lesser", j0, width)
+            nc.vector.tensor_tensor(out=lesser[:], in0=deleted[:], in1=inserted[:], op=ALU.min)
+            size = keep.tile([P, width, PACK], BF16, name="z_size%d" % j0, align_bytes=64)
+            nc.vector.tensor_tensor(out=woven(size[:]), in0=unwoven(lesser[:]), in1=unwoven(sub[:]), op=ALU.min)
+            z = keep.tile([P, width, PACK], BF16, name="z%d" % j0, align_bytes=64)
+            nc.vector.tensor_tensor(out=z[:], in0=size[:], in1=gain_sign[:, :width, :], op=ALU.mult)
+            z_scales = keep.tile([P, width], U8, name="z_scales%d" % j0, align_bytes=64)
+            z_words = quantise(z, j0, width, "z", z_scales[:])
+            return product(w4, z_words[:], z_scales[:], width, "out")
+
+        def hand_out(banks, j0, width):
+            result = rows_tile("result", j0, width)
+            for t0, count, bank in banks:
+                nc.scalar.copy(out=result[:, t0 : t0 + count, :], in_=bank[:])
+            nc.sync.dma_start(out_rows[:, :, j0 : j0 + width], result[:])
+            rounded = keep.tile([P, width, PACK], BF16, name="rounded%d" % j0, align_bytes=64)
+            nc.vector.tensor_copy(out=woven(rounded[:]), in_=unwoven(result[:]))
+            words = quantise(rounded, j0, width, "out", out_scales[:, j0 : j0 + width])
+            nc.sync.dma_start(out_words[:, j0 : j0 + width], words[:].bitcast(I32))
+
+        pending = None
+        for j0, width in CHUNKS:
+            gap = symbol_gap(j0, width)
+            cost = substitution_cost(gap, j0, width)
+            deleted = fetch(del_t, "deleted", j0, width)
+            inserted = fetch(ins_t, "inserted", j0, width)
+            sub = substituted(cost, j0, width)
+            if pending is not None:
+                hand_out(*pending)
+            pending = (cell(deleted, inserted, sub, j0, width), j0, width)
+        hand_out(*pending)
+        for q in range(4):
+            queue = nc.sync if q % 2 == 0 else nc.scalar
+            queue.dma_start(out_2[0, 4 * q : 4 * q + 4, :].bitcast(I32), out_scales[32 * q : 32 * q + 4, :].bitcast(I32))

@@ -21,9 +21,13 @@ F = 512
 HALF = 256
 LIST_ROWS = 16
 CHUNKS = [(0, 128), (128, 128), (256, 128), (384, 128)]
-WIDEST = 128
+GAP_PIECES = [(0, 256), (256, 256)]
+COST_PIECES = {0: 256, 256: 256}
+FETCH_PIECES = {0: 256, 256: 128, 384: 128}
+VECTOR_FETCHES = [("inserted", 0, t) for t in range(4)]
+SCALAR_WEAVES = [0, 128]
 
-REUSE = {"c_x_words0": "w2_scale_raw", "y_x_words0": "w1_scale_raw", "bent0": "y_x_words1"}
+REUSE = {"y_x_scales": "w2_scale_raw", "bent": "y_x_words0"}
 
 FLOPS = 4 * 2 * 512 * 512 * 512
 
@@ -50,10 +54,15 @@ def tile_picked_editcell_none_po_kernel(
                 rows = src[0, 4 * q : 4 * q + 4, :].bitcast(I32)
                 queues[q].dma_start(tile[32 * q : 32 * q + 32, :].bitcast(I32), rows.unsqueeze(0).to_broadcast([8] + list(rows.shape)))
 
+        def load_scale_rows(tile, src):
+            for q in range(4):
+                nc.sync.dma_start(tile[32 * q : 32 * q + 4, :].bitcast(I32), src[0, 4 * q : 4 * q + 4, :].bitcast(I32))
+
         x_scale_table = keep.tile([P, T], U8, name="x_scale_table", align_bytes=64)
         w_scale_raw = {}
-        for name in ("w1", "w3", "w2", "w4"):
+        for name in ("w3", "w2", "w1", "w4"):
             w_scale_raw[name] = keep.tile([P, F], U8, name=name + "_scale_raw", tag=name + "_scale_raw", align_bytes=64)
+            nc.gpsimd.memset(w_scale_raw[name][:].bitcast(I32), 0)
 
         def load_words(name, words):
             raw = keep.tile([P, 2 * F], U8, name=name + "_word_raw", align_bytes=64)
@@ -75,31 +84,31 @@ def tile_picked_editcell_none_po_kernel(
 
         load_scale_rows_everywhere([nc.sync, nc.sync, nc.scalar, nc.scalar], x_scale_table, x_scales)
         thr_t = load_list(thr, "thr_t")
+        two_t = load_list(two, "two_t")
         w3_raw = load_words("w3", w3_words)
         x_word_table = keep.tile([P, T], I32, name="x_word_table", tag="x_word_table", align_bytes=64)
         nc.sync.dma_start(x_word_table[:], x_words[0].rearrange("p n t -> p (n t)").bitcast(I32))
-        load_scale_rows_everywhere([nc.sync] * 4, w_scale_raw["w3"], w3_scales)
+        load_scale_rows(w_scale_raw["w3"], w3_scales)
         w2_raw = load_words("w2", w2_words)
-        load_scale_rows_everywhere([nc.sync] * 4, w_scale_raw["w2"], w2_scales)
-        two_t = load_list(two, "two_t")
         w1_raw = load_words("w1", w1_words)
+        w4_raw = load_words("w4", w4_words)
+        load_scale_rows(w_scale_raw["w2"], w2_scales)
+        offs_t = load_list(offs, "offs_t")
+        load_scale_rows(w_scale_raw["w1"], w1_scales)
+        sym_t = load_list(sym_l, "sym_t")
         gain = keep.tile([P, PACK], F32, name="gain")
         nc.sync.dma_start(gain[:], gn.rearrange("(p t) o -> p (t o)", t=PACK))
-        load_scale_rows_everywhere([nc.sync] * 4, w_scale_raw["w1"], w1_scales)
-        offs_t = load_list(offs, "offs_t")
-        sym_t = load_list(sym_l, "sym_t")
-        w4_raw = load_words("w4", w4_words)
         del_t = load_list(del_l, "del_t")
         ins_t = load_list(ins_l, "ins_t")
         sub_t = load_list(sub_l, "sub_t")
-        load_scale_rows_everywhere([nc.sync] * 4, w_scale_raw["w4"], w4_scales)
+        load_scale_rows(w_scale_raw["w4"], w4_scales)
 
         gain_size = keep.tile([P, PACK], F32, name="gain_size")
         nc.scalar.activation(out=gain_size[:], in_=gain[:], func=ACT.Abs)
         half_gain_size = keep.tile([P, PACK], F32, name="half_gain_size")
         nc.scalar.activation(out=half_gain_size[:], in_=gain[:], func=ACT.Abs, scale=0.5)
-        gain_sign = keep.tile([P, WIDEST, PACK], BF16, name="gain_sign", align_bytes=64)
-        nc.scalar.activation(out=gain_sign[:], in_=gain[:].unsqueeze(1).to_broadcast([P, WIDEST, PACK]), func=ACT.Sign)
+        gain_sign = keep.tile([P, PACK], BF16, name="gain_sign", align_bytes=64)
+        nc.scalar.activation(out=gain_sign[:], in_=gain[:], func=ACT.Sign)
 
         def product(weight, words, scales, width, name):
             w_words, w_scales = weight
@@ -121,40 +130,54 @@ def tile_picked_editcell_none_po_kernel(
                 results.append((t0, per_bank, bank))
             return results
 
-        def picked_product(lst, weight, name, empty):
-            scales = keep.tile([P, S], U8, name=name + "_x_scales", align_bytes=64)
+        def picked_scales(lst, name):
+            scales = keep.tile([P, S], U8, name=name + "_x_scales", tag=REUSE.get(name + "_x_scales", name + "_x_scales"), align_bytes=64)
             nc.vector.tensor_copy(out=scales[:], in_=x_scale_table[:].indirect(lst[:]))
-            for h in range(S // HALF):
-                words = keep.tile([P, HALF], U32, name="%s_x_words%d" % (name, h), tag=REUSE.get("%s_x_words%d" % (name, h), "%s_x_words%d" % (name, h)), align_bytes=64)
-                nc.vector.tensor_copy(out=words[:], in_=x_word_table[:].bitcast(U32).indirect(entries(lst, h * HALF, HALF)))
-                for t0, count, bank in product(weight, words[:], scales[:, h * HALF : (h + 1) * HALF], HALF, name):
-                    empty(h, t0, count, bank)
+            return scales
+
+        def picked_product(lst, scales, weight, name, width, empty):
+            for j0 in range(0, S, width):
+                own = "%s_x_words%d" % (name, j0)
+                words = keep.tile([P, width], U32, name=own, tag=REUSE.get(own, own), align_bytes=64)
+                nc.vector.tensor_copy(out=words[:], in_=x_word_table[:].bitcast(U32).indirect(entries(lst, j0, width)))
+                for t0, count, bank in product(weight, words[:], scales[:, j0 : j0 + width], width, name):
+                    empty(j0, width, t0, count, bank)
 
         y_rows = [keep.tile([P, S], F32, name="y_rows%d" % t) for t in range(PACK)]
         d_rows = [keep.tile([P, S], F32, name="d_rows%d" % t) for t in range(PACK)]
         c_rows = keep.tile([P, PACK, S], F32, name="c_rows")
 
-        def empty_y(h, t0, count, bank):
+        def empty_y(j0, width, t0, count, bank):
             for i in range(count):
                 t = t0 + i
                 nc.scalar.activation(
-                    out=y_rows[t][:, h * HALF : (h + 1) * HALF], in_=bank[:, i, :], func=ACT.Identity,
+                    out=y_rows[t][:, j0 : j0 + width], in_=bank[:, i, :], func=ACT.Identity,
                     scale=gain_size[:, t : t + 1], bias=half_gain_size[:, t : t + 1],
                 )
 
-        def empty_d(h, t0, count, bank):
+        def empty_d(j0, width, t0, count, bank):
             for i in range(count):
-                nc.scalar.copy(out=d_rows[t0 + i][:, h * HALF : (h + 1) * HALF], in_=bank[:, i, :])
+                nc.scalar.copy(out=d_rows[t0 + i][:, j0 : j0 + width], in_=bank[:, i, :])
 
-        def empty_c(h, t0, count, bank):
-            nc.scalar.copy(out=c_rows[:, t0 : t0 + count, h * HALF : (h + 1) * HALF], in_=bank[:])
+        def empty_c(j0, width, t0, count, bank):
+            nc.scalar.copy(out=c_rows[:, t0 : t0 + count, j0 : j0 + width], in_=bank[:])
 
-        picked_product(thr_t, deal_weight("w3", w3_raw), "d", empty_d)
-        picked_product(two_t, deal_weight("w2", w2_raw), "c", empty_c)
-        picked_product(offs_t, deal_weight("w1", w1_raw), "y", empty_y)
+        d_scales = picked_scales(thr_t, "d")
+        c_scales = picked_scales(two_t, "c")
+        picked_product(thr_t, d_scales, deal_weight("w3", w3_raw), "d", HALF, empty_d)
+        picked_product(two_t, c_scales, deal_weight("w2", w2_raw), "c", S, empty_c)
+        picked_product(offs_t, picked_scales(offs_t, "y"), deal_weight("w1", w1_raw), "y", S, empty_y)
         w4 = deal_weight("w4", w4_raw)
 
-        gaps = keep.tile([P, len(CHUNKS), PACK, WIDEST], F32, name="gaps", tag="x_word_table", align_bytes=64)
+        def all_rows(name, tag):
+            return keep.tile([P, PACK, S], F32, name=name, tag=tag, align_bytes=64)
+
+        gaps = all_rows("gaps", "x_word_table")
+        bent = all_rows("bent", "y_x_words0")
+        cost = all_rows("cost", "cost")
+        sub = all_rows("sub", "sub")
+        deleted = all_rows("deleted", "deleted")
+        inserted = all_rows("inserted", "inserted")
         out_scales = keep.tile([P, S], U8, name="out_scales", align_bytes=64)
         out_rows = out_0.rearrange("(p t) j -> p t j", t=PACK)
         out_words = out_1[0].rearrange("p n t -> p (n t)").bitcast(I32)
@@ -164,58 +187,52 @@ def tile_picked_editcell_none_po_kernel(
             return keep.tile([P, PACK, width], F32, name=own, tag=REUSE.get(own, own), align_bytes=64)
 
         def woven(ap):
-            return ap.rearrange("p (c i) t -> p c t i", i=4)
+            return ap.rearrange("p (c i) t -> p c t i", i=2)
 
         def unwoven(ap):
-            return ap.rearrange("p t (c i) -> p c t i", i=4)
+            return ap.rearrange("p t (c i) -> p c t i", i=2)
 
         def symbol_gap(j0, width):
-            gap = gaps[:, j0 // width, :, :]
             for t in range(PACK):
                 nc.vector.tensor_tensor(
-                    out=gap[:, t, :], in0=d_rows[t][:].indirect(entries(sym_t, j0, width)),
+                    out=gaps[:, t, j0 : j0 + width], in0=d_rows[t][:].indirect(entries(sym_t, j0, width)),
                     in1=c_rows[:, t, j0 : j0 + width], op=ALU.subtract,
                 )
-            return gap
 
-        def substitution_cost(gap, j0, width):
-            bent = rows_tile("bent", j0, width)
-            nc.scalar.activation(out=bent[:], in_=gap, func=ACT.Tanh, scale=0.5)
-            cost = rows_tile("cost", j0, width)
+        def substitution_cost(j0, width):
+            cols = slice(j0, j0 + width)
+            nc.scalar.activation(out=bent[:, :, cols], in_=gaps[:, :, cols], func=ACT.Tanh, scale=0.5)
             for t in range(PACK):
-                nc.scalar.activation(out=cost[:, t, :], in_=bent[:, t, :], func=ACT.Abs, scale=half_gain_size[:, t : t + 1])
-            return cost
+                nc.scalar.activation(out=cost[:, t, cols], in_=bent[:, t, cols], func=ACT.Abs, scale=half_gain_size[:, t : t + 1])
 
-        def fetch(lst, name, j0, width):
-            got = rows_tile(name, j0, width)
+        def fetch(lst, got, name, j0, width):
             for t in range(PACK):
                 window = y_rows[t][:].indirect(entries(lst, j0, width))
-                if (name, j0) == ("inserted", 384):
-                    nc.vector.tensor_copy(out=got[:, t, :], in_=window)
+                if (name, j0, t) in VECTOR_FETCHES:
+                    nc.vector.tensor_copy(out=got[:, t, j0 : j0 + width], in_=window)
                 else:
-                    nc.scalar.activation(out=got[:, t, :], in_=window, func=ACT.Copy)
-            return got
+                    nc.scalar.activation(out=got[:, t, j0 : j0 + width], in_=window, func=ACT.Copy)
 
-        def substituted(cost, j0, width):
-            got = rows_tile("sub", j0, width)
+        def substituted(j0, width):
             for t in range(PACK):
                 nc.vector.tensor_tensor(
-                    out=got[:, t, :], in0=y_rows[t][:].indirect(entries(sub_t, j0, width)), in1=cost[:, t, :], op=ALU.add,
+                    out=sub[:, t, j0 : j0 + width], in0=y_rows[t][:].indirect(entries(sub_t, j0, width)),
+                    in1=cost[:, t, j0 : j0 + width], op=ALU.add,
                 )
-            return got
 
         def quantise(values, j0, width, name, scales):
             words = keep.tile([P, width], U32, name="%s_words%d" % (name, j0), align_bytes=64)
             nc.vector.quantize_mx(out=words[:].bitcast(FP8X4), scales=scales, in_=values[:].rearrange("p j t -> p (j t)"))
             return words
 
-        def cell(deleted, inserted, sub, j0, width):
+        def cell(j0, width):
+            cols = slice(j0, j0 + width)
             lesser = rows_tile("lesser", j0, width)
-            nc.vector.tensor_tensor(out=lesser[:], in0=deleted[:], in1=inserted[:], op=ALU.min)
+            nc.vector.tensor_tensor(out=lesser[:], in0=deleted[:, :, cols], in1=inserted[:, :, cols], op=ALU.min)
             size = keep.tile([P, width, PACK], BF16, name="z_size%d" % j0, align_bytes=64)
-            nc.vector.tensor_tensor(out=woven(size[:]), in0=unwoven(lesser[:]), in1=unwoven(sub[:]), op=ALU.min)
+            nc.vector.tensor_tensor(out=woven(size[:]), in0=unwoven(lesser[:]), in1=unwoven(sub[:, :, cols]), op=ALU.min)
             z = keep.tile([P, width, PACK], BF16, name="z%d" % j0, align_bytes=64)
-            nc.vector.tensor_tensor(out=z[:], in0=size[:], in1=gain_sign[:, :width, :], op=ALU.mult)
+            nc.vector.tensor_tensor(out=z[:], in0=size[:], in1=gain_sign[:].unsqueeze(1).to_broadcast([P, width, PACK]), op=ALU.mult)
             z_scales = keep.tile([P, width], U8, name="z_scales%d" % j0, align_bytes=64)
             z_words = quantise(z, j0, width, "z", z_scales[:])
             return product(w4, z_words[:], z_scales[:], width, "out")
@@ -226,21 +243,27 @@ def tile_picked_editcell_none_po_kernel(
                 nc.scalar.copy(out=result[:, t0 : t0 + count, :], in_=bank[:])
             nc.sync.dma_start(out_rows[:, :, j0 : j0 + width], result[:])
             rounded = keep.tile([P, width, PACK], BF16, name="rounded%d" % j0, align_bytes=64)
-            nc.vector.tensor_copy(out=woven(rounded[:]), in_=unwoven(result[:]))
+            if j0 in SCALAR_WEAVES:
+                nc.scalar.copy(out=rounded[:], in_=banks[0][2][:].rearrange("p t j -> p j t"))
+            else:
+                nc.vector.tensor_copy(out=woven(rounded[:]), in_=unwoven(result[:]))
             words = quantise(rounded, j0, width, "out", out_scales[:, j0 : j0 + width])
             nc.sync.dma_start(out_words[:, j0 : j0 + width], words[:].bitcast(I32))
 
-        pending = None
+        for j0, width in GAP_PIECES:
+            symbol_gap(j0, width)
+        all_banks = []
         for j0, width in CHUNKS:
-            gap = symbol_gap(j0, width)
-            cost = substitution_cost(gap, j0, width)
-            deleted = fetch(del_t, "deleted", j0, width)
-            inserted = fetch(ins_t, "inserted", j0, width)
-            sub = substituted(cost, j0, width)
-            if pending is not None:
-                hand_out(*pending)
-            pending = (cell(deleted, inserted, sub, j0, width), j0, width)
-        hand_out(*pending)
+            if j0 in COST_PIECES:
+                substitution_cost(j0, COST_PIECES[j0])
+            if j0 in FETCH_PIECES:
+                fetch(del_t, deleted, "deleted", j0, FETCH_PIECES[j0])
+                fetch(ins_t, inserted, "inserted", j0, FETCH_PIECES[j0])
+            if j0 in COST_PIECES:
+                substituted(j0, COST_PIECES[j0])
+            all_banks.append(cell(j0, width))
+        for banks, (j0, width) in zip(all_banks, CHUNKS):
+            hand_out(banks, j0, width)
         for q in range(4):
             queue = nc.sync if q % 2 == 0 else nc.scalar
             queue.dma_start(out_2[0, 4 * q : 4 * q + 4, :].bitcast(I32), out_scales[32 * q : 32 * q + 4, :].bitcast(I32))

@@ -23,11 +23,12 @@ LIST_ROWS = 16
 CHUNKS = [(0, 128), (128, 128), (256, 128), (384, 128)]
 GAP_PIECES = [(0, 256), (256, 256)]
 COST_PIECES = {0: 256, 256: 256}
+SUB_PIECES = {0: 256, 256: 128, 384: 128}
 FETCH_PIECES = {0: 256, 256: 128, 384: 128}
-VECTOR_FETCHES = [("inserted", 0, t) for t in range(4)]
-SCALAR_WEAVES = [0, 128]
+VECTOR_FETCHES = [("inserted", 0, t) for t in range(3)]
+SCALAR_WEAVES = [0, 128, 256]
 
-REUSE = {"y_x_scales": "w2_scale_raw", "bent": "y_x_words0"}
+REUSE = {"y_x_scales": "w2_scale_raw", "d_x_words256": "w3_scale_raw", "c_x_words0": "w2_word_raw"}
 
 FLOPS = 4 * 2 * 512 * 512 * 512
 
@@ -65,22 +66,28 @@ def tile_picked_editcell_none_po_kernel(
             nc.gpsimd.memset(w_scale_raw[name][:].bitcast(I32), 0)
 
         def load_words(name, words):
-            raw = keep.tile([P, 2 * F], U8, name=name + "_word_raw", align_bytes=64)
+            raw = keep.tile([P, 2 * F], U8, name=name + "_word_raw", tag=name + "_word_raw", align_bytes=64)
             nc.sync.dma_start(raw[:].bitcast(I32), words[0].bitcast(I32))
             return raw
 
-        def deal_weight(name, raw):
+        def deal_words(name, raw):
             words = keep.tile([P, 2 * F], U8, name=name + "_words", align_bytes=64)
             nc.scalar.copy(
                 out=words[:].bitcast(U16).rearrange("p (t m) -> p t m", t=PACK),
                 in_=raw[:].bitcast(U16).rearrange("p (m t) -> p t m", t=PACK),
             )
+            return words
+
+        def deal_scales(name):
             scales = keep.tile([P, F], U8, name=name + "_scales", align_bytes=64)
             nc.vector.tensor_copy(
                 out=scales[:].rearrange("p (t m) -> p t m", t=PACK),
                 in_=w_scale_raw[name][:].rearrange("p (m t) -> p t m", t=PACK),
             )
-            return words, scales
+            return scales
+
+        def deal_weight(name, raw):
+            return deal_words(name, raw), deal_scales(name)
 
         load_scale_rows_everywhere([nc.sync, nc.sync, nc.scalar, nc.scalar], x_scale_table, x_scales)
         thr_t = load_list(thr, "thr_t")
@@ -112,7 +119,7 @@ def tile_picked_editcell_none_po_kernel(
 
         def product(weight, words, scales, width, name):
             w_words, w_scales = weight
-            per_bank = 512 // width
+            per_bank = 512 // width if name != "last" else 2
             results = []
             for t0 in range(0, PACK, per_bank):
                 bank = psum.tile([P, per_bank, width], F32, name="bank")
@@ -220,34 +227,41 @@ def tile_picked_editcell_none_po_kernel(
                     in1=cost[:, t, j0 : j0 + width], op=ALU.add,
                 )
 
-        def quantise(values, j0, width, name, scales):
-            words = keep.tile([P, width], U32, name="%s_words%d" % (name, j0), align_bytes=64)
-            nc.vector.quantize_mx(out=words[:].bitcast(FP8X4), scales=scales, in_=values[:].rearrange("p j t -> p (j t)"))
-            return words
+        def quantise(values, words, scales):
+            nc.vector.quantize_mx(out=words.bitcast(FP8X4), scales=scales, in_=values.rearrange("p j t -> p (j t)"))
 
-        def cell(j0, width):
-            cols = slice(j0, j0 + width)
+        def cell(j0, width, step):
             lesser = rows_tile("lesser", j0, width)
-            nc.vector.tensor_tensor(out=lesser[:], in0=deleted[:, :, cols], in1=inserted[:, :, cols], op=ALU.min)
             size = keep.tile([P, width, PACK], BF16, name="z_size%d" % j0, align_bytes=64)
-            nc.vector.tensor_tensor(out=woven(size[:]), in0=unwoven(lesser[:]), in1=unwoven(sub[:, :, cols]), op=ALU.min)
-            z = keep.tile([P, width, PACK], BF16, name="z%d" % j0, align_bytes=64)
-            nc.vector.tensor_tensor(out=z[:], in0=size[:], in1=gain_sign[:].unsqueeze(1).to_broadcast([P, width, PACK]), op=ALU.mult)
+            z = keep.tile([P, width, PACK], BF16, name="z%d" % j0, tag="z%d" % j0, align_bytes=64)
+            z_words = keep.tile([P, width], U32, name="z_words%d" % j0, align_bytes=64)
             z_scales = keep.tile([P, width], U8, name="z_scales%d" % j0, align_bytes=64)
-            z_words = quantise(z, j0, width, "z", z_scales[:])
-            return product(w4, z_words[:], z_scales[:], width, "out")
+            parts = [(slice(a, a + step), slice(j0 + a, j0 + a + step)) for a in range(0, width, step)]
+            for part, cols in parts:
+                nc.vector.tensor_tensor(out=lesser[:, :, part], in0=deleted[:, :, cols], in1=inserted[:, :, cols], op=ALU.min)
+            for part, cols in parts:
+                nc.vector.tensor_tensor(out=woven(size[:, part, :]), in0=unwoven(lesser[:, :, part]), in1=unwoven(sub[:, :, cols]), op=ALU.min)
+            for part, cols in parts:
+                nc.vector.tensor_tensor(
+                    out=z[:, part, :], in0=size[:, part, :], in1=gain_sign[:].unsqueeze(1).to_broadcast([P, step, PACK]), op=ALU.mult,
+                )
+            for part, cols in parts:
+                quantise(z[:, part, :], z_words[:, part], z_scales[:, part])
+            return product(w4, z_words[:], z_scales[:], width, "last" if j0 == 384 and True else "out")
 
-        def hand_out(banks, j0, width):
+        def hand_out(banks, j0, width, rounded):
             result = rows_tile("result", j0, width)
             for t0, count, bank in banks:
                 nc.scalar.copy(out=result[:, t0 : t0 + count, :], in_=bank[:])
             nc.sync.dma_start(out_rows[:, :, j0 : j0 + width], result[:])
-            rounded = keep.tile([P, width, PACK], BF16, name="rounded%d" % j0, align_bytes=64)
             if j0 in SCALAR_WEAVES:
-                nc.scalar.copy(out=rounded[:], in_=banks[0][2][:].rearrange("p t j -> p j t"))
+                nc.scalar.copy(out=rounded, in_=banks[0][2][:].rearrange("p t j -> p j t"))
             else:
-                nc.vector.tensor_copy(out=woven(rounded[:]), in_=unwoven(result[:]))
-            words = quantise(rounded, j0, width, "out", out_scales[:, j0 : j0 + width])
+                nc.vector.tensor_copy(out=woven(rounded), in_=unwoven(result[:]))
+
+        def hand_out_planes(rounded, j0, width, tag):
+            words = keep.tile([P, width], U32, name="out_words%d" % j0, tag=tag, align_bytes=64)
+            quantise(rounded, words[:], out_scales[:, j0 : j0 + width])
             nc.sync.dma_start(out_words[:, j0 : j0 + width], words[:].bitcast(I32))
 
         for j0, width in GAP_PIECES:
@@ -259,11 +273,16 @@ def tile_picked_editcell_none_po_kernel(
             if j0 in FETCH_PIECES:
                 fetch(del_t, deleted, "deleted", j0, FETCH_PIECES[j0])
                 fetch(ins_t, inserted, "inserted", j0, FETCH_PIECES[j0])
-            if j0 in COST_PIECES:
-                substituted(j0, COST_PIECES[j0])
-            all_banks.append(cell(j0, width))
-        for banks, (j0, width) in zip(all_banks, CHUNKS):
-            hand_out(banks, j0, width)
+            if j0 in SUB_PIECES:
+                substituted(j0, SUB_PIECES[j0])
+            all_banks.append(cell(j0, width, 64 if j0 == 384 else width))
+        early = keep.tile([P, 384, PACK], BF16, name="rounded_early", align_bytes=64)
+        late = keep.tile([P, 128, PACK], BF16, name="rounded_late", align_bytes=64)
+        for k in range(3):
+            hand_out(all_banks[k], *CHUNKS[k], early[:, 128 * k : 128 * (k + 1), :])
+        hand_out_planes(early[:], 0, 384, "z384")
+        hand_out(all_banks[3], *CHUNKS[3], late[:])
+        hand_out_planes(late[:], 384, 128, "out_words384")
         for q in range(4):
             queue = nc.sync if q % 2 == 0 else nc.scalar
             queue.dma_start(out_2[0, 4 * q : 4 * q + 4, :].bitcast(I32), out_scales[32 * q : 32 * q + 4, :].bitcast(I32))

@@ -14,21 +14,19 @@ ACT = mybir.ActivationFunctionType
 ALU = mybir.AluOpType
 
 P = 128
-PACK = 4
-T = 2048
-S = 512
-F = 512
-HALF = 256
-LIST_ROWS = 16
-CHUNKS = [(0, 128), (128, 128), (256, 128), (384, 128)]
-GAP_PIECES = [(0, 256), (256, 256)]
-COST_PIECES = {0: 256, 256: 256}
-SUB_PIECES = {0: 256, 256: 128, 384: 128}
-FETCH_PIECES = {0: 256, 256: 128, 384: 128}
-VECTOR_FETCHES = [("inserted", 0, t) for t in range(3)]
-SCALAR_WEAVES = [0, 128, 256]
+SLOTS = 4
+QUADRANTS = 4
+SYMBOLS = 2048
+PLACES = 512
+FEATURES = 512
+GROUP = 16
+BANK = 512
+HALF = PLACES // 2
+QUARTER = PLACES // 4
 
-REUSE = {"y_x_scales": "w2_scale_raw", "d_x_words256": "w3_scale_raw", "c_x_words0": "w2_word_raw"}
+STRETCHES = [(0, HALF), (HALF, QUARTER), (HALF + QUARTER, QUARTER)]
+VECTOR_INSERT_SLOTS = 3
+LAST_CELL_PART = QUARTER // 2
 
 FLOPS = 4 * 2 * 512 * 512 * 512
 
@@ -42,247 +40,234 @@ def tile_picked_editcell_none_po_kernel(
         keep = ctx.enter_context(tc.tile_pool(name="keep", bufs=1))
         psum = ctx.enter_context(tc.psum_pool(name="psum", bufs=8))
 
+        def sbuf(shape, dtype, name, reuses=None):
+            return keep.tile(shape, dtype, name=name, tag=reuses or name, align_bytes=64)
+
         def load_list(src, name):
-            tile = keep.tile([P, S // LIST_ROWS], U16, name=name)
-            nc.sync.dma_start(tile[:], src)
-            return tile
+            offsets = keep.tile([P, PLACES // GROUP], U16, name=name)
+            nc.sync.dma_start(offsets[:], src)
+            return offsets
 
-        def entries(lst, start, width):
-            return lst[:, start // LIST_ROWS : (start + width) // LIST_ROWS]
+        def entries(offsets, start, width):
+            return offsets[:, start // GROUP : (start + width) // GROUP]
 
-        def load_scale_rows_everywhere(queues, tile, src):
-            for q in range(4):
-                rows = src[0, 4 * q : 4 * q + 4, :].bitcast(I32)
-                queues[q].dma_start(tile[32 * q : 32 * q + 32, :].bitcast(I32), rows.unsqueeze(0).to_broadcast([8] + list(rows.shape)))
-
-        def load_scale_rows(tile, src):
-            for q in range(4):
-                nc.sync.dma_start(tile[32 * q : 32 * q + 4, :].bitcast(I32), src[0, 4 * q : 4 * q + 4, :].bitcast(I32))
-
-        x_scale_table = keep.tile([P, T], U8, name="x_scale_table", align_bytes=64)
-        w_scale_raw = {}
-        for name in ("w3", "w2", "w1", "w4"):
-            w_scale_raw[name] = keep.tile([P, F], U8, name=name + "_scale_raw", tag=name + "_scale_raw", align_bytes=64)
-            nc.gpsimd.memset(w_scale_raw[name][:].bitcast(I32), 0)
-
-        def load_words(name, words):
-            raw = keep.tile([P, 2 * F], U8, name=name + "_word_raw", tag=name + "_word_raw", align_bytes=64)
+        def load_weight_words(name, words):
+            raw = sbuf([P, 2 * FEATURES], U8, name + "_word_raw")
             nc.sync.dma_start(raw[:].bitcast(I32), words[0].bitcast(I32))
             return raw
 
-        def deal_words(name, raw):
-            words = keep.tile([P, 2 * F], U8, name=name + "_words", align_bytes=64)
-            nc.scalar.copy(
-                out=words[:].bitcast(U16).rearrange("p (t m) -> p t m", t=PACK),
-                in_=raw[:].bitcast(U16).rearrange("p (m t) -> p t m", t=PACK),
+        def load_weight_scales(name, scales):
+            for q in range(QUADRANTS):
+                nc.sync.dma_start(
+                    scale_raw[name][32 * q : 32 * q + 4, :].bitcast(I32), scales[0, 4 * q : 4 * q + 4, :].bitcast(I32)
+                )
+
+        x_scale_table = sbuf([P, SYMBOLS], U8, "x_scale_table")
+        scale_raw = {}
+        for name in ("w3", "w2", "w1", "w4"):
+            scale_raw[name] = sbuf([P, FEATURES], U8, name + "_scale_raw")
+            nc.gpsimd.memset(scale_raw[name][:].bitcast(I32), 0)
+
+        for q, queue in enumerate((nc.sync, nc.sync, nc.scalar, nc.scalar)):
+            rows = x_scales[0, 4 * q : 4 * q + 4, :].bitcast(I32)
+            queue.dma_start(
+                x_scale_table[32 * q : 32 * q + 32, :].bitcast(I32), rows.unsqueeze(0).to_broadcast([8, 4, SYMBOLS // 4])
             )
-            return words
-
-        def deal_scales(name):
-            scales = keep.tile([P, F], U8, name=name + "_scales", align_bytes=64)
-            nc.vector.tensor_copy(
-                out=scales[:].rearrange("p (t m) -> p t m", t=PACK),
-                in_=w_scale_raw[name][:].rearrange("p (m t) -> p t m", t=PACK),
-            )
-            return scales
-
-        def deal_weight(name, raw):
-            return deal_words(name, raw), deal_scales(name)
-
-        load_scale_rows_everywhere([nc.sync, nc.sync, nc.scalar, nc.scalar], x_scale_table, x_scales)
         thr_t = load_list(thr, "thr_t")
         two_t = load_list(two, "two_t")
-        w3_raw = load_words("w3", w3_words)
-        x_word_table = keep.tile([P, T], I32, name="x_word_table", tag="x_word_table", align_bytes=64)
+        x_word_table = sbuf([P, SYMBOLS], I32, "x_word_table")
         nc.sync.dma_start(x_word_table[:], x_words[0].rearrange("p n t -> p (n t)").bitcast(I32))
-        load_scale_rows(w_scale_raw["w3"], w3_scales)
-        w2_raw = load_words("w2", w2_words)
-        w1_raw = load_words("w1", w1_words)
-        w4_raw = load_words("w4", w4_words)
-        load_scale_rows(w_scale_raw["w2"], w2_scales)
+        w3_raw = load_weight_words("w3", w3_words)
+        load_weight_scales("w3", w3_scales)
+        w2_raw = load_weight_words("w2", w2_words)
+        w1_raw = load_weight_words("w1", w1_words)
+        load_weight_scales("w2", w2_scales)
         offs_t = load_list(offs, "offs_t")
-        load_scale_rows(w_scale_raw["w1"], w1_scales)
+        load_weight_scales("w1", w1_scales)
         sym_t = load_list(sym_l, "sym_t")
-        gain = keep.tile([P, PACK], F32, name="gain")
-        nc.sync.dma_start(gain[:], gn.rearrange("(p t) o -> p (t o)", t=PACK))
+        gain = keep.tile([P, SLOTS], F32, name="gain")
+        nc.sync.dma_start(gain[:], gn.rearrange("(p t) o -> p (t o)", t=SLOTS))
+        w4_raw = load_weight_words("w4", w4_words)
         del_t = load_list(del_l, "del_t")
         ins_t = load_list(ins_l, "ins_t")
         sub_t = load_list(sub_l, "sub_t")
-        load_scale_rows(w_scale_raw["w4"], w4_scales)
+        load_weight_scales("w4", w4_scales)
 
-        gain_size = keep.tile([P, PACK], F32, name="gain_size")
+        gain_size = keep.tile([P, SLOTS], F32, name="gain_size")
         nc.scalar.activation(out=gain_size[:], in_=gain[:], func=ACT.Abs)
-        half_gain_size = keep.tile([P, PACK], F32, name="half_gain_size")
+        half_gain_size = keep.tile([P, SLOTS], F32, name="half_gain_size")
         nc.scalar.activation(out=half_gain_size[:], in_=gain[:], func=ACT.Abs, scale=0.5)
-        gain_sign = keep.tile([P, PACK], BF16, name="gain_sign", align_bytes=64)
+        gain_sign = sbuf([P, SLOTS], BF16, "gain_sign")
         nc.scalar.activation(out=gain_sign[:], in_=gain[:], func=ACT.Sign)
 
-        def product(weight, words, scales, width, name):
-            w_words, w_scales = weight
-            per_bank = 512 // width if name != "last" else 2
-            results = []
-            for t0 in range(0, PACK, per_bank):
-                bank = psum.tile([P, per_bank, width], F32, name="bank")
-                for i in range(per_bank):
+        def deal_weight(name, raw):
+            words = sbuf([P, 2 * FEATURES], U8, name + "_words")
+            nc.scalar.copy(
+                out=words[:].bitcast(U16).rearrange("p (t m) -> p t m", t=SLOTS),
+                in_=raw[:].bitcast(U16).rearrange("p (m t) -> p t m", t=SLOTS),
+            )
+            scales = sbuf([P, FEATURES], U8, name + "_scales")
+            nc.vector.tensor_copy(
+                out=scales[:].rearrange("p (t m) -> p t m", t=SLOTS),
+                in_=scale_raw[name][:].rearrange("p (m t) -> p t m", t=SLOTS),
+            )
+            return words, scales
+
+        def product(weight, words, scales, slots_per_bank):
+            weight_words, weight_scales = weight
+            banks = []
+            for t0 in range(0, SLOTS, slots_per_bank):
+                bank = psum.tile([P, slots_per_bank, words.shape[1]], F32, name="bank")
+                for i in range(slots_per_bank):
                     t = t0 + i
                     nc.tensor.matmul_mx(
                         out=bank[:, i, :],
-                        lhsT=w_words[:, 2 * P * t : 2 * P * (t + 1)].bitcast(FP4X4),
-                        lhsT_scale=w_scales[:, P * t : P * (t + 1)],
+                        lhsT=weight_words[:, 2 * P * t : 2 * P * (t + 1)].bitcast(FP4X4),
+                        lhsT_scale=weight_scales[:, P * t : P * (t + 1)],
                         rhs=words.bitcast(FP8X4),
                         rhs_scale=scales,
                         start=True,
                         stop=True,
                     )
-                results.append((t0, per_bank, bank))
-            return results
+                banks.append((t0, bank))
+            return banks
 
-        def picked_scales(lst, name):
-            scales = keep.tile([P, S], U8, name=name + "_x_scales", tag=REUSE.get(name + "_x_scales", name + "_x_scales"), align_bytes=64)
-            nc.vector.tensor_copy(out=scales[:], in_=x_scale_table[:].indirect(lst[:]))
+        def picked_scales(offsets, name, reuses=None):
+            scales = sbuf([P, PLACES], U8, name, reuses)
+            nc.vector.tensor_copy(out=scales[:], in_=x_scale_table[:].indirect(offsets[:]))
             return scales
 
-        def picked_product(lst, scales, weight, name, width, empty):
-            for j0 in range(0, S, width):
-                own = "%s_x_words%d" % (name, j0)
-                words = keep.tile([P, width], U32, name=own, tag=REUSE.get(own, own), align_bytes=64)
-                nc.vector.tensor_copy(out=words[:], in_=x_word_table[:].bitcast(U32).indirect(entries(lst, j0, width)))
-                for t0, count, bank in product(weight, words[:], scales[:, j0 : j0 + width], width, name):
-                    empty(j0, width, t0, count, bank)
+        def picked_product(offsets, scales, weight, start, width, name, reuses=None):
+            words = sbuf([P, width], U32, name, reuses)
+            nc.vector.tensor_copy(out=words[:], in_=x_word_table[:].bitcast(U32).indirect(entries(offsets, start, width)))
+            return product(weight, words[:], scales[:, start : start + width], BANK // width)
 
-        y_rows = [keep.tile([P, S], F32, name="y_rows%d" % t) for t in range(PACK)]
-        d_rows = [keep.tile([P, S], F32, name="d_rows%d" % t) for t in range(PACK)]
-        c_rows = keep.tile([P, PACK, S], F32, name="c_rows")
+        y_rows = [keep.tile([P, PLACES], F32, name="y_rows%d" % t) for t in range(SLOTS)]
+        d_rows = [keep.tile([P, PLACES], F32, name="d_rows%d" % t) for t in range(SLOTS)]
+        c_rows = keep.tile([P, SLOTS, PLACES], F32, name="c_rows")
 
-        def empty_y(j0, width, t0, count, bank):
-            for i in range(count):
-                t = t0 + i
-                nc.scalar.activation(
-                    out=y_rows[t][:, j0 : j0 + width], in_=bank[:, i, :], func=ACT.Identity,
-                    scale=gain_size[:, t : t + 1], bias=half_gain_size[:, t : t + 1],
-                )
-
-        def empty_d(j0, width, t0, count, bank):
-            for i in range(count):
-                nc.scalar.copy(out=d_rows[t0 + i][:, j0 : j0 + width], in_=bank[:, i, :])
-
-        def empty_c(j0, width, t0, count, bank):
-            nc.scalar.copy(out=c_rows[:, t0 : t0 + count, j0 : j0 + width], in_=bank[:])
-
-        d_scales = picked_scales(thr_t, "d")
-        c_scales = picked_scales(two_t, "c")
-        picked_product(thr_t, d_scales, deal_weight("w3", w3_raw), "d", HALF, empty_d)
-        picked_product(two_t, c_scales, deal_weight("w2", w2_raw), "c", S, empty_c)
-        picked_product(offs_t, picked_scales(offs_t, "y"), deal_weight("w1", w1_raw), "y", S, empty_y)
+        d_x_scales = picked_scales(thr_t, "d_x_scales")
+        c_x_scales = picked_scales(two_t, "c_x_scales")
+        w3 = deal_weight("w3", w3_raw)
+        for start, reuses in ((0, None), (HALF, "w3_scale_raw")):
+            for t0, bank in picked_product(thr_t, d_x_scales, w3, start, HALF, "d_x_words%d" % start, reuses):
+                for i in range(BANK // HALF):
+                    nc.scalar.copy(out=d_rows[t0 + i][:, start : start + HALF], in_=bank[:, i, :])
+        w2 = deal_weight("w2", w2_raw)
+        for t, bank in picked_product(two_t, c_x_scales, w2, 0, PLACES, "c_x_words", "w2_word_raw"):
+            nc.scalar.copy(out=c_rows[:, t : t + 1, :], in_=bank[:])
+        y_x_scales = picked_scales(offs_t, "y_x_scales", "w2_scale_raw")
+        w1 = deal_weight("w1", w1_raw)
+        for t, bank in picked_product(offs_t, y_x_scales, w1, 0, PLACES, "y_x_words"):
+            nc.scalar.activation(
+                out=y_rows[t][:], in_=bank[:, 0, :], func=ACT.Identity,
+                scale=gain_size[:, t : t + 1], bias=half_gain_size[:, t : t + 1],
+            )
         w4 = deal_weight("w4", w4_raw)
 
-        def all_rows(name, tag):
-            return keep.tile([P, PACK, S], F32, name=name, tag=tag, align_bytes=64)
-
-        gaps = all_rows("gaps", "x_word_table")
-        bent = all_rows("bent", "y_x_words0")
-        cost = all_rows("cost", "cost")
-        sub = all_rows("sub", "sub")
-        deleted = all_rows("deleted", "deleted")
-        inserted = all_rows("inserted", "inserted")
-        out_scales = keep.tile([P, S], U8, name="out_scales", align_bytes=64)
-        out_rows = out_0.rearrange("(p t) j -> p t j", t=PACK)
+        gaps = sbuf([P, SLOTS, PLACES], F32, "gaps", "x_word_table")
+        bent = sbuf([P, SLOTS, PLACES], F32, "bent", "y_x_words")
+        cost = sbuf([P, SLOTS, PLACES], F32, "cost")
+        substituted = sbuf([P, SLOTS, PLACES], F32, "substituted")
+        deleted = sbuf([P, SLOTS, PLACES], F32, "deleted")
+        inserted = sbuf([P, SLOTS, PLACES], F32, "inserted")
+        out_scales = sbuf([P, PLACES], U8, "out_scales")
+        out_rows = out_0.rearrange("(p t) j -> p t j", t=SLOTS)
         out_words = out_1[0].rearrange("p n t -> p (n t)").bitcast(I32)
 
-        def rows_tile(name, j0, width):
-            own = "%s%d" % (name, j0)
-            return keep.tile([P, PACK, width], F32, name=own, tag=REUSE.get(own, own), align_bytes=64)
-
-        def woven(ap):
+        def slots_inside(ap):
             return ap.rearrange("p (c i) t -> p c t i", i=2)
 
-        def unwoven(ap):
+        def slots_outside(ap):
             return ap.rearrange("p t (c i) -> p c t i", i=2)
-
-        def symbol_gap(j0, width):
-            for t in range(PACK):
-                nc.vector.tensor_tensor(
-                    out=gaps[:, t, j0 : j0 + width], in0=d_rows[t][:].indirect(entries(sym_t, j0, width)),
-                    in1=c_rows[:, t, j0 : j0 + width], op=ALU.subtract,
-                )
-
-        def substitution_cost(j0, width):
-            cols = slice(j0, j0 + width)
-            nc.scalar.activation(out=bent[:, :, cols], in_=gaps[:, :, cols], func=ACT.Tanh, scale=0.5)
-            for t in range(PACK):
-                nc.scalar.activation(out=cost[:, t, cols], in_=bent[:, t, cols], func=ACT.Abs, scale=half_gain_size[:, t : t + 1])
-
-        def fetch(lst, got, name, j0, width):
-            for t in range(PACK):
-                window = y_rows[t][:].indirect(entries(lst, j0, width))
-                if (name, j0, t) in VECTOR_FETCHES:
-                    nc.vector.tensor_copy(out=got[:, t, j0 : j0 + width], in_=window)
-                else:
-                    nc.scalar.activation(out=got[:, t, j0 : j0 + width], in_=window, func=ACT.Copy)
-
-        def substituted(j0, width):
-            for t in range(PACK):
-                nc.vector.tensor_tensor(
-                    out=sub[:, t, j0 : j0 + width], in0=y_rows[t][:].indirect(entries(sub_t, j0, width)),
-                    in1=cost[:, t, j0 : j0 + width], op=ALU.add,
-                )
 
         def quantise(values, words, scales):
             nc.vector.quantize_mx(out=words.bitcast(FP8X4), scales=scales, in_=values.rearrange("p j t -> p (j t)"))
 
-        def cell(j0, width, step):
-            lesser = rows_tile("lesser", j0, width)
-            size = keep.tile([P, width, PACK], BF16, name="z_size%d" % j0, align_bytes=64)
-            z = keep.tile([P, width, PACK], BF16, name="z%d" % j0, tag="z%d" % j0, align_bytes=64)
-            z_words = keep.tile([P, width], U32, name="z_words%d" % j0, align_bytes=64)
-            z_scales = keep.tile([P, width], U8, name="z_scales%d" % j0, align_bytes=64)
-            parts = [(slice(a, a + step), slice(j0 + a, j0 + a + step)) for a in range(0, width, step)]
+        def substitution_cost(start, width):
+            cols = slice(start, start + width)
+            nc.scalar.activation(out=bent[:, :, cols], in_=gaps[:, :, cols], func=ACT.Tanh, scale=0.5)
+            for t in range(SLOTS):
+                nc.scalar.activation(out=cost[:, t, cols], in_=bent[:, t, cols], func=ACT.Abs, scale=half_gain_size[:, t : t + 1])
+
+        def look_up_y(offsets, into, start, width, vector_slots):
+            for t in range(SLOTS):
+                window = y_rows[t][:].indirect(entries(offsets, start, width))
+                if t < vector_slots:
+                    nc.vector.tensor_copy(out=into[:, t, start : start + width], in_=window)
+                else:
+                    nc.scalar.activation(out=into[:, t, start : start + width], in_=window, func=ACT.Copy)
+
+        def substitute(start, width):
+            for t in range(SLOTS):
+                nc.vector.tensor_tensor(
+                    out=substituted[:, t, start : start + width], in0=y_rows[t][:].indirect(entries(sub_t, start, width)),
+                    in1=cost[:, t, start : start + width], op=ALU.add,
+                )
+
+        def cells(start, width, part_width):
+            lesser = sbuf([P, SLOTS, width], F32, "lesser%d" % start)
+            least = sbuf([P, width, SLOTS], BF16, "least%d" % start)
+            z = sbuf([P, width, SLOTS], BF16, "z%d" % start)
+            z_words = sbuf([P, width], U32, "z_words%d" % start)
+            z_scales = sbuf([P, width], U8, "z_scales%d" % start)
+            parts = [(slice(a, a + part_width), slice(start + a, start + a + part_width)) for a in range(0, width, part_width)]
+            signs = gain_sign[:].unsqueeze(1).to_broadcast([P, part_width, SLOTS])
             for part, cols in parts:
                 nc.vector.tensor_tensor(out=lesser[:, :, part], in0=deleted[:, :, cols], in1=inserted[:, :, cols], op=ALU.min)
             for part, cols in parts:
-                nc.vector.tensor_tensor(out=woven(size[:, part, :]), in0=unwoven(lesser[:, :, part]), in1=unwoven(sub[:, :, cols]), op=ALU.min)
-            for part, cols in parts:
                 nc.vector.tensor_tensor(
-                    out=z[:, part, :], in0=size[:, part, :], in1=gain_sign[:].unsqueeze(1).to_broadcast([P, step, PACK]), op=ALU.mult,
+                    out=slots_inside(least[:, part, :]), in0=slots_outside(lesser[:, :, part]),
+                    in1=slots_outside(substituted[:, :, cols]), op=ALU.min,
                 )
             for part, cols in parts:
+                nc.vector.tensor_tensor(out=z[:, part, :], in0=least[:, part, :], in1=signs, op=ALU.mult)
+            for part, cols in parts:
                 quantise(z[:, part, :], z_words[:, part], z_scales[:, part])
-            return product(w4, z_words[:], z_scales[:], width, "last" if j0 == 384 and True else "out")
+            return z_words, z_scales
 
-        def hand_out(banks, j0, width, rounded):
-            result = rows_tile("result", j0, width)
-            for t0, count, bank in banks:
-                nc.scalar.copy(out=result[:, t0 : t0 + count, :], in_=bank[:])
-            nc.sync.dma_start(out_rows[:, :, j0 : j0 + width], result[:])
-            if j0 in SCALAR_WEAVES:
-                nc.scalar.copy(out=rounded, in_=banks[0][2][:].rearrange("p t j -> p j t"))
-            else:
-                nc.vector.tensor_copy(out=woven(rounded), in_=unwoven(result[:]))
+        def store_result(banks, start):
+            result = sbuf([P, SLOTS, QUARTER], F32, "result%d" % start)
+            for t0, bank in banks:
+                nc.scalar.copy(out=result[:, t0 : t0 + bank.shape[1], :], in_=bank[:])
+            nc.sync.dma_start(out_rows[:, :, start : start + QUARTER], result[:])
+            return result
 
-        def hand_out_planes(rounded, j0, width, tag):
-            words = keep.tile([P, width], U32, name="out_words%d" % j0, tag=tag, align_bytes=64)
-            quantise(rounded, words[:], out_scales[:, j0 : j0 + width])
-            nc.sync.dma_start(out_words[:, j0 : j0 + width], words[:].bitcast(I32))
+        for start in (0, HALF):
+            for t in range(SLOTS):
+                nc.vector.tensor_tensor(
+                    out=gaps[:, t, start : start + HALF], in0=d_rows[t][:].indirect(entries(sym_t, start, HALF)),
+                    in1=c_rows[:, t, start : start + HALF], op=ALU.subtract,
+                )
 
-        for j0, width in GAP_PIECES:
-            symbol_gap(j0, width)
-        all_banks = []
-        for j0, width in CHUNKS:
-            if j0 in COST_PIECES:
-                substitution_cost(j0, COST_PIECES[j0])
-            if j0 in FETCH_PIECES:
-                fetch(del_t, deleted, "deleted", j0, FETCH_PIECES[j0])
-                fetch(ins_t, inserted, "inserted", j0, FETCH_PIECES[j0])
-            if j0 in SUB_PIECES:
-                substituted(j0, SUB_PIECES[j0])
-            all_banks.append(cell(j0, width, 64 if j0 == 384 else width))
-        early = keep.tile([P, 384, PACK], BF16, name="rounded_early", align_bytes=64)
-        late = keep.tile([P, 128, PACK], BF16, name="rounded_late", align_bytes=64)
-        for k in range(3):
-            hand_out(all_banks[k], *CHUNKS[k], early[:, 128 * k : 128 * (k + 1), :])
-        hand_out_planes(early[:], 0, 384, "z384")
-        hand_out(all_banks[3], *CHUNKS[3], late[:])
-        hand_out_planes(late[:], 384, 128, "out_words384")
-        for q in range(4):
-            queue = nc.sync if q % 2 == 0 else nc.scalar
+        last_start = STRETCHES[-1][0]
+        out_banks = []
+        for start, width in STRETCHES:
+            last = start == last_start
+            substitution_cost(start, width)
+            look_up_y(del_t, deleted, start, width, 0)
+            look_up_y(ins_t, inserted, start, width, VECTOR_INSERT_SLOTS if start == 0 else 0)
+            substitute(start, width)
+            z_words, z_scales = cells(start, width, LAST_CELL_PART if last else width)
+            for a in range(0, width, QUARTER):
+                out_banks.append(product(w4, z_words[:, a : a + QUARTER], z_scales[:, a : a + QUARTER], SLOTS // 2 if last else SLOTS))
+
+        early = sbuf([P, HALF, SLOTS], BF16, "rounded_early")
+        late = sbuf([P, HALF, SLOTS], BF16, "rounded_late", "least%d" % last_start)
+        for k in range(2):
+            store_result(out_banks[k], QUARTER * k)
+            whole_bank = out_banks[k][0][1]
+            nc.scalar.copy(out=early[:, QUARTER * k : QUARTER * (k + 1), :], in_=whole_bank[:].rearrange("p t j -> p j t"))
+        early_words = sbuf([P, HALF], U32, "early_words", "z%d" % last_start)
+        quantise(early[:], early_words[:], out_scales[:, :HALF])
+        nc.sync.dma_start(out_words[:, :HALF], early_words[:].bitcast(I32))
+        late_words = sbuf([P, HALF], U32, "late_words")
+        for k in range(2):
+            part = slice(QUARTER * k, QUARTER * (k + 1))
+            start = HALF + QUARTER * k
+            result = store_result(out_banks[2 + k], start)
+            nc.vector.tensor_copy(out=slots_inside(late[:, part, :]), in_=slots_outside(result[:]))
+            quantise(late[:, part, :], late_words[:, part], out_scales[:, start : start + QUARTER])
+        nc.sync.dma_start(out_words[:, HALF:], late_words[:].bitcast(I32))
+        for q, queue in enumerate((nc.sync, nc.scalar, nc.sync, nc.scalar)):
             queue.dma_start(out_2[0, 4 * q : 4 * q + 4, :].bitcast(I32), out_scales[32 * q : 32 * q + 4, :].bitcast(I32))

from contextlib import ExitStack

import concourse.mybir as mybir

F32 = mybir.dt.float32
BF16 = mybir.dt.bfloat16
I32 = mybir.dt.int32
U32 = mybir.dt.uint32
U16 = mybir.dt.uint16
U8 = mybir.dt.uint8
FP8X4 = mybir.dt.float8_e4m3fn_x4
FP4X4 = mybir.dt.float4_e2m1fn_x4
ACT = mybir.ActivationFunctionType
ALU = mybir.AluOpType

P = 128
SLOTS = 4
QUADRANTS = 4
SYMBOLS = 2048
PLACES = 512
FEATURES = 512
GROUP = 16
BANK = 512
HALF = PLACES // 2
QUARTER = PLACES // 4

STRETCHES = [(0, HALF), (HALF, QUARTER), (HALF + QUARTER, QUARTER)]
VECTOR_INSERT_SLOTS = 3
LAST_CELL_PART = QUARTER // 2

FLOPS = 4 * 2 * 512 * 512 * 512


def tile_picked_editcell_none_po_kernel(
    tc, x_words, x_scales, w1_words, w1_scales, w2_words, w2_scales, w3_words, w3_scales, gn,
    w4_words, w4_scales, offs, two, thr, sym_l, del_l, ins_l, sub_l, out_0, out_1, out_2,
):
    nc = tc.nc
    with ExitStack() as ctx:
        keep = ctx.enter_context(tc.tile_pool(name="keep", bufs=1))
        psum = ctx.enter_context(tc.psum_pool(name="psum", bufs=8))

        def sbuf(shape, dtype, name, reuses=None):
            return keep.tile(shape, dtype, name=name, tag=reuses or name, align_bytes=64)

        def load_list(src, name):
            offsets = keep.tile([P, PLACES // GROUP], U16, name=name)
            nc.sync.dma_start(offsets[:], src)
            return offsets

        def entries(offsets, start, width):
            return offsets[:, start // GROUP : (start + width) // GROUP]

        def load_weight_words(name, words):
            raw = sbuf([P, 2 * FEATURES], U8, name + "_word_raw")
            nc.sync.dma_start(raw[:].bitcast(I32), words[0].bitcast(I32))
            return raw

        def load_weight_scales(name, scales):
            for q in range(QUADRANTS):
                nc.sync.dma_start(
                    scale_raw[name][32 * q : 32 * q + 4, :].bitcast(I32), scales[0, 4 * q : 4 * q + 4, :].bitcast(I32)
                )

        x_scale_table = sbuf([P, SYMBOLS], U8, "x_scale_table")
        scale_raw = {}
        for name in ("w3", "w2", "w1", "w4"):
            scale_raw[name] = sbuf([P, FEATURES], U8, name + "_scale_raw")
            nc.gpsimd.memset(scale_raw[name][:].bitcast(I32), 0)

        for q, queue in enumerate((nc.sync, nc.sync, nc.scalar, nc.scalar)):
            rows = x_scales[0, 4 * q : 4 * q + 4, :].bitcast(I32)
            queue.dma_start(
                x_scale_table[32 * q : 32 * q + 32, :].bitcast(I32), rows.unsqueeze(0).to_broadcast([8, 4, SYMBOLS // 4])
            )
        thr_t = load_list(thr, "thr_t")
        two_t = load_list(two, "two_t")
        x_word_table = sbuf([P, SYMBOLS], I32, "x_word_table")
        nc.sync.dma_start(x_word_table[:], x_words[0].rearrange("p n t -> p (n t)").bitcast(I32))
        w3_raw = load_weight_words("w3", w3_words)
        load_weight_scales("w3", w3_scales)
        w2_raw = load_weight_words("w2", w2_words)
        w1_raw = load_weight_words("w1", w1_words)
        load_weight_scales("w2", w2_scales)
        offs_t = load_list(offs, "offs_t")
        load_weight_scales("w1", w1_scales)
        sym_t = load_list(sym_l, "sym_t")
        gain = keep.tile([P, SLOTS], F32, name="gain")
        nc.sync.dma_start(gain[:], gn.rearrange("(p t) o -> p (t o)", t=SLOTS))
        w4_raw = load_weight_words("w4", w4_words)
        del_t = load_list(del_l, "del_t")
        ins_t = load_list(ins_l, "ins_t")
        sub_t = load_list(sub_l, "sub_t")
        load_weight_scales("w4", w4_scales)

        gain_size = keep.tile([P, SLOTS], F32, name="gain_size")
        nc.scalar.activation(out=gain_size[:], in_=gain[:], func=ACT.Abs)
        half_gain_size = keep.tile([P, SLOTS], F32, name="half_gain_size")
        nc.scalar.activation(out=half_gain_size[:], in_=gain[:], func=ACT.Abs, scale=0.5)
        gain_sign = sbuf([P, SLOTS], BF16, "gain_sign")
        nc.scalar.activation(out=gain_sign[:], in_=gain[:], func=ACT.Sign)

        def deal_weight(name, raw):
            words = sbuf([P, 2 * FEATURES], U8, name + "_words")
            nc.scalar.copy(
                out=words[:].bitcast(U16).rearrange("p (t m) -> p t m", t=SLOTS),
                in_=raw[:].bitcast(U16).rearrange("p (m t) -> p t m", t=SLOTS),
            )
            scales = sbuf([P, FEATURES], U8, name + "_scales")
            nc.vector.tensor_copy(
                out=scales[:].rearrange("p (t m) -> p t m", t=SLOTS),
                in_=scale_raw[name][:].rearrange("p (m t) -> p t m", t=SLOTS),
            )
            return words, scales

        def product(weight, words, scales, slots_per_bank):
            weight_words, weight_scales = weight
            banks = []
            for t0 in range(0, SLOTS, slots_per_bank):
                bank = psum.tile([P, slots_per_bank, words.shape[1]], F32, name="bank")
                for i in range(slots_per_bank):
                    t = t0 + i
                    nc.tensor.matmul_mx(
                        out=bank[:, i, :],
                        lhsT=weight_words[:, 2 * P * t : 2 * P * (t + 1)].bitcast(FP4X4),
                        lhsT_scale=weight_scales[:, P * t : P * (t + 1)],
                        rhs=words.bitcast(FP8X4),
                        rhs_scale=scales,
                        start=True,
                        stop=True,
                    )
                banks.append((t0, bank))
            return banks

        def picked_scales(offsets, name, reuses=None):
            scales = sbuf([P, PLACES], U8, name, reuses)
            nc.vector.tensor_copy(out=scales[:], in_=x_scale_table[:].indirect(offsets[:]))
            return scales

        def picked_product(offsets, scales, weight, start, width, name, reuses=None):
            words = sbuf([P, width], U32, name, reuses)
            nc.vector.tensor_copy(out=words[:], in_=x_word_table[:].bitcast(U32).indirect(entries(offsets, start, width)))
            return product(weight, words[:], scales[:, start : start + width], BANK // width)

        y_rows = [keep.tile([P, PLACES], F32, name="y_rows%d" % t) for t in range(SLOTS)]
        d_rows = [keep.tile([P, PLACES], F32, name="d_rows%d" % t) for t in range(SLOTS)]
        c_rows = keep.tile([P, SLOTS, PLACES], F32, name="c_rows")

        d_x_scales = picked_scales(thr_t, "d_x_scales")
        c_x_scales = picked_scales(two_t, "c_x_scales")
        w3 = deal_weight("w3", w3_raw)
        for start, reuses in ((0, None), (HALF, "w3_scale_raw")):
            for t0, bank in picked_product(thr_t, d_x_scales, w3, start, HALF, "d_x_words%d" % start, reuses):
                for i in range(BANK // HALF):
                    nc.scalar.copy(out=d_rows[t0 + i][:, start : start + HALF], in_=bank[:, i, :])
        w2 = deal_weight("w2", w2_raw)
        for t, bank in picked_product(two_t, c_x_scales, w2, 0, PLACES, "c_x_words", "w2_word_raw"):
            nc.scalar.copy(out=c_rows[:, t : t + 1, :], in_=bank[:])
        y_x_scales = picked_scales(offs_t, "y_x_scales", "w2_scale_raw")
        w1 = deal_weight("w1", w1_raw)
        for t, bank in picked_product(offs_t, y_x_scales, w1, 0, PLACES, "y_x_words"):
            nc.scalar.activation(
                out=y_rows[t][:], in_=bank[:, 0, :], func=ACT.Identity,
                scale=gain_size[:, t : t + 1], bias=half_gain_size[:, t : t + 1],
            )
        w4 = deal_weight("w4", w4_raw)

        gaps = sbuf([P, SLOTS, PLACES], F32, "gaps", "x_word_table")
        bent = sbuf([P, SLOTS, PLACES], F32, "bent", "y_x_words")
        cost = sbuf([P, SLOTS, PLACES], F32, "cost")
        substituted = sbuf([P, SLOTS, PLACES], F32, "substituted")
        deleted = sbuf([P, SLOTS, PLACES], F32, "deleted")
        inserted = sbuf([P, SLOTS, PLACES], F32, "inserted")
        out_scales = sbuf([P, PLACES], U8, "out_scales")
        out_rows = out_0.rearrange("(p t) j -> p t j", t=SLOTS)
        out_words = out_1[0].rearrange("p n t -> p (n t)").bitcast(I32)

        def slots_inside(ap):
            return ap.rearrange("p (c i) t -> p c t i", i=2)

        def slots_outside(ap):
            return ap.rearrange("p t (c i) -> p c t i", i=2)

        def quantise(values, words, scales):
            nc.vector.quantize_mx(out=words.bitcast(FP8X4), scales=scales, in_=values.rearrange("p j t -> p (j t)"))

        def substitution_cost(start, width):
            cols = slice(start, start + width)
            nc.scalar.activation(out=bent[:, :, cols], in_=gaps[:, :, cols], func=ACT.Tanh, scale=0.5)
            for t in range(SLOTS):
                nc.scalar.activation(out=cost[:, t, cols], in_=bent[:, t, cols], func=ACT.Abs, scale=half_gain_size[:, t : t + 1])

        def look_up_y(offsets, into, start, width, vector_slots):
            for t in range(SLOTS):
                window = y_rows[t][:].indirect(entries(offsets, start, width))
                if t < vector_slots:
                    nc.vector.tensor_copy(out=into[:, t, start : start + width], in_=window)
                else:
                    nc.scalar.activation(out=into[:, t, start : start + width], in_=window, func=ACT.Copy)

        def substitute(start, width):
            for t in range(SLOTS):
                nc.vector.tensor_tensor(
                    out=substituted[:, t, start : start + width], in0=y_rows[t][:].indirect(entries(sub_t, start, width)),
                    in1=cost[:, t, start : start + width], op=ALU.add,
                )

        def cells(start, width, part_width):
            lesser = sbuf([P, SLOTS, width], F32, "lesser%d" % start)
            least = sbuf([P, width, SLOTS], BF16, "least%d" % start)
            z = sbuf([P, width, SLOTS], BF16, "z%d" % start)
            z_words = sbuf([P, width], U32, "z_words%d" % start)
            z_scales = sbuf([P, width], U8, "z_scales%d" % start)
            parts = [(slice(a, a + part_width), slice(start + a, start + a + part_width)) for a in range(0, width, part_width)]
            signs = gain_sign[:].unsqueeze(1).to_broadcast([P, part_width, SLOTS])
            for part, cols in parts:
                nc.vector.tensor_tensor(out=lesser[:, :, part], in0=deleted[:, :, cols], in1=inserted[:, :, cols], op=ALU.min)
            for part, cols in parts:
                nc.vector.tensor_tensor(
                    out=slots_inside(least[:, part, :]), in0=slots_outside(lesser[:, :, part]),
                    in1=slots_outside(substituted[:, :, cols]), op=ALU.min,
                )
            for part, cols in parts:
                nc.vector.tensor_tensor(out=z[:, part, :], in0=least[:, part, :], in1=signs, op=ALU.mult)
            for part, cols in parts:
                quantise(z[:, part, :], z_words[:, part], z_scales[:, part])
            return z_words, z_scales

        def store_result(banks, start):
            result = sbuf([P, SLOTS, QUARTER], F32, "result%d" % start)
            for t0, bank in banks:
                nc.scalar.copy(out=result[:, t0 : t0 + bank.shape[1], :], in_=bank[:])
            nc.sync.dma_start(out_rows[:, :, start : start + QUARTER], result[:])
            return result

        for start in (0, HALF):
            for t in range(SLOTS):
                nc.vector.tensor_tensor(
                    out=gaps[:, t, start : start + HALF], in0=d_rows[t][:].indirect(entries(sym_t, start, HALF)),
                    in1=c_rows[:, t, start : start + HALF], op=ALU.subtract,
                )

        last_start = STRETCHES[-1][0]
        out_banks = []
        for start, width in STRETCHES:
            last = start == last_start
            substitution_cost(start, width)
            look_up_y(del_t, deleted, start, width, 0)
            look_up_y(ins_t, inserted, start, width, VECTOR_INSERT_SLOTS if start == 0 else 0)
            substitute(start, width)
            z_words, z_scales = cells(start, width, LAST_CELL_PART if last else width)
            for a in range(0, width, QUARTER):
                out_banks.append(product(w4, z_words[:, a : a + QUARTER], z_scales[:, a : a + QUARTER], SLOTS // 2 if last else SLOTS))

        early = sbuf([P, HALF, SLOTS], BF16, "rounded_early")
        late = sbuf([P, HALF, SLOTS], BF16, "rounded_late", "least%d" % last_start)
        for k in range(2):
            store_result(out_banks[k], QUARTER * k)
            whole_bank = out_banks[k][0][1]
            nc.scalar.copy(out=early[:, QUARTER * k : QUARTER * (k + 1), :], in_=whole_bank[:].rearrange("p t j -> p j t"))
        early_words = sbuf([P, HALF], U32, "early_words", "z%d" % last_start)
        quantise(early[:], early_words[:], out_scales[:, :HALF])
        nc.sync.dma_start(out_words[:, :HALF], early_words[:].bitcast(I32))
        late_words = sbuf([P, HALF], U32, "late_words")
        for k in range(2):
            part = slice(QUARTER * k, QUARTER * (k + 1))
            start = HALF + QUARTER * k
            result = store_result(out_banks[2 + k], start)
            nc.vector.tensor_copy(out=slots_inside(late[:, part, :]), in_=slots_outside(result[:]))
            quantise(late[:, part, :], late_words[:, part], out_scales[:, start : start + QUARTER])
        nc.sync.dma_start(out_words[:, HALF:], late_words[:].bitcast(I32))
        for q, queue in enumerate((nc.sync, nc.scalar, nc.sync, nc.scalar)):
            queue.dma_start(out_2[0, 4 * q : 4 * q + 4, :].bitcast(I32), out_scales[32 * q : 32 * q + 4, :].bitcast(I32))
